import numpy as np
import ml_dtypes


def mxq(x, axis, fmt="e4m3"):
    dtype, down = {"e4m3": (ml_dtypes.float8_e4m3fn, 7), "e5m2": (ml_dtypes.float8_e5m2, 14)}[fmt]
    v = np.moveaxis(np.asarray(x, np.float32).astype(ml_dtypes.bfloat16).astype(np.float64), axis, -1)
    blocks = v.reshape(v.shape[:-1] + (-1, 32))
    amax = np.abs(blocks).max(-1, keepdims=True)
    byte = np.maximum(np.where(amax > 0, np.frexp(amax)[1] - 1 + 127, 0) - down, 1)
    scale = np.exp2(byte - 127.0)
    codes = (blocks / scale).astype(np.float32).astype(dtype).astype(np.float64)
    return np.moveaxis((codes * scale).reshape(v.shape), -1, axis)


WIDE = False


def mx_kscale(k):
    if not WIDE:
        return np.ones(k)
    levels = np.array([10, -10, 5, -5, 0])
    if k % 512:
        return np.exp2(np.random.permutation(np.resize(levels, k // 32))).repeat(32)
    a = np.empty((k // 512, 16))
    for p in range(k // 512):
        a[p, :8] = np.random.permutation(np.resize(levels, 8))
        for g in range(8):
            far = levels[np.abs(levels - a[p, g]) >= 10]
            a[p, g + 8] = far[np.random.randint(len(far))]
    return np.exp2(a.ravel()).repeat(32)


BF16 = ml_dtypes.bfloat16


def bf(x):
    return np.asarray(x, np.float32).astype(BF16)


def f64(x):
    return np.asarray(x).astype(np.float64)


E2M1 = np.array([0.0, 0.5, 1.0, 1.5, 2.0, 3.0, 4.0, 6.0, -0.0, -0.5, -1.0, -1.5, -2.0, -3.0, -4.0, -6.0])


def pack_weight(w, fmt):
    k, n = w.shape
    w = f64(bf(w)).reshape(k // 32, 32, n)
    amax = np.abs(w).max(1)
    if fmt == "e4m3":
        byte = np.frexp(amax)[1] - 1 + 127 - 7
    else:
        mant, ex = np.frexp(amax / 6.0)
        byte = np.where(mant > 0.5, ex, ex - 1) + 127
    byte = np.clip(np.where(amax > 0, byte, 1), 1, 254)
    scaled = (w * np.exp2(127.0 - byte)[:, None, :]).reshape(k, n).astype(np.float32)
    by_word = np.ascontiguousarray(scaled.reshape(k // 512, 128, 4, n).transpose(0, 1, 3, 2))
    if fmt == "e4m3":
        words = by_word.astype(ml_dtypes.float8_e4m3fn).view(np.uint8)
    else:
        c = by_word.astype(ml_dtypes.float4_e2m1fn).view(np.uint8) & 0xF
        words = c[..., 0::2] | (c[..., 1::2] << 4)
    return np.ascontiguousarray(words), np.ascontiguousarray(byte.astype(np.uint8).reshape(k // 512, 16, n))


def unpack_weight(words, scales, fmt):
    g, p, n, _ = words.shape
    if fmt == "e4m3":
        vals = np.ascontiguousarray(words).view(ml_dtypes.float8_e4m3fn).astype(np.float64)
    else:
        nib = np.empty((g, p, n, 4), np.uint8)
        nib[..., 0::2] = words & 0xF
        nib[..., 1::2] = words >> 4
        vals = E2M1[nib]
    vals = vals * np.repeat(np.exp2(scales.astype(np.float64) - 127.0), 8, axis=1)[..., None]
    return vals.transpose(0, 1, 3, 2).reshape(g * 512, n)
def pack4(w):
    words, scales = pack_weight(w, "e2m1")
    return words.reshape(words.shape[0], 128, -1), scales


def unpack4(words, scales):
    return unpack_weight(words.reshape(words.shape[0], 128, -1, 2), scales, "e2m1")


E4M3FN = np.array([(-1.0 if i & 128 else 1.0) * ((1.0 + (i & 7) / 8.0) * 2.0 ** (((i >> 3) & 15) - 7) if i & 120 else (i & 7) * 2.0 ** -9) for i in range(256)])


def e4m3fn_bytes(y):
    return np.clip(np.asarray(y, np.float64), -448.0, 448.0).astype(np.float32).astype(ml_dtypes.float8_e4m3fn).view(np.uint8)


def e4m3fn_values(b):
    return E4M3FN[b]


N, M, K, L = 1024, 1024, 512, 1024


def positive_root(s, m):
    return 0.5 * (np.sqrt(s * s + 4.0 * m) - s)


def draw0():
    s = mx_kscale(K)
    u = mx_kscale(N)
    r = np.random.uniform(0.5, 1.3, (N, 1))
    x = bf(np.random.standard_normal((N, K)) * r * s)
    beta = np.random.standard_normal((M, K)) * (1.2 / np.sqrt(K)) / s
    beta_words, beta_scales = pack4(beta.T)
    return {
        "x": x,
        "beta_words": beta_words,
        "beta_scales": beta_scales,
        "bs": bf(np.random.uniform(0.5, 1.5, M)),
        "mass": bf(np.random.uniform(0.5, 2.0, N)),
        "obs": bf(np.random.uniform(0.0, 1.6, (N, M))),
        "wt": bf((1.0 + 0.1 * np.random.standard_normal(N)) * u),
        "z": bf(np.random.standard_normal((N, L)) / np.sqrt(N) / u[:, None]),
    }


def core(x, beta_words, beta_scales, bs, mass, obs, wt, z):
    phi = mxq(f64(x), 1, "e4m3") @ unpack4(beta_words, beta_scales)
    e = f64(bs)[None, :] * np.exp(0.5 * phi)
    sn = np.mean(e, axis=1)
    a = positive_root(sn, f64(mass))
    fit = a[:, None] * e
    res = f64(wt)[:, None] * (f64(obs) - fit)
    return mxq(f64(z), 0, "e4m3").T @ mxq(res, 0, "e4m3")


def setup_inputs():
    drawn = draw0()
    full = np.asarray(drawn['z']).astype(np.float64)
    scale = (np.abs(full).reshape(1024, 8, 128).max(axis=(2,)) / 448.0).astype(np.float32)
    given = {}
    for key, value in drawn.items():
        if key == 'z':
            given['z_bytes'] = e4m3fn_bytes(full / np.repeat(scale.astype(np.float64), 128, axis=1))
            given['z_scale'] = scale
        else:
            given[key] = value
    return given


def reference(x, beta_words, beta_scales, bs, mass, obs, wt, z_bytes, z_scale):
    return core(x, beta_words, beta_scales, bs, mass, obs, wt, e4m3fn_values(z_bytes) * np.repeat(z_scale.astype(np.float64), 128, axis=1))

@@ -1,0 +1,486 @@
+from contextlib import ExitStack
+
+import concourse.mybir as mybir
+from concourse.masks import make_identity
+
+N, M, K, L = 1024, 1024, 512, 1024
+FLOPS = 2 * N * M * K + 2 * L * M * N
+
+F32 = mybir.dt.float32
+BF16 = mybir.dt.bfloat16
+I32 = mybir.dt.int32
+U32 = mybir.dt.uint32
+U8 = mybir.dt.uint8
+FP8 = mybir.dt.float8_e4m3fn
+FP8X4 = mybir.dt.float8_e4m3fn_x4
+FP4X4 = mybir.dt.float4_e2m1fn_x4
+ALU = mybir.AluOpType
+ACT = mybir.ActivationFunctionType
+
+P = 128
+T = 4
+G = 2
+HALF = 512
+QUART = 256
+
+PLAN = [
+    ("xt", "T", 0),
+    ("zw", "A", 0, 0),
+    ("zw", "V", 0, 1),
+    ("zi", "V", 0, 0),
+    ("zw", "A", 0, 2),
+    ("zi", "V", 0, 1),
+    ("xt", "T", 1),
+    ("zw", "V", 0, 3),
+    ("xe", "A", 0),
+    ("zi", "V", 0, 2),
+    ("zw", "V", 1, 0),
+    ("xq", "V", 0),
+    ("zi", "V", 1, 0),
+    ("bs", "T"),
+    ("m1", "T", 0, 0),
+    ("xt", "T", 2),
+    ("zw", "V", 1, 1),
+    ("xe", "A", 1),
+    ("xq", "V", 1),
+    ("zw", "A", 1, 2),
+    ("ex", "A", 0, 0),
+    ("m1", "T", 0, 1),
+    ("ex", "A", 0, 1),
+    ("zq", "V", 0, 0),
+    ("m1", "T", 1, 0),
+    ("zq", "V", 0, 1),
+    ("xe", "V", 2),
+    ("zq", "V", 0, 2),
+    ("m1", "T", 1, 1),
+    ("m1", "T", 2, 0),
+    ("ex", "A", 1, 0),
+    ("zq", "V", 1, 0),
+    ("xt", "T", 3),
+    ("m1", "T", 2, 1),
+    ("ex", "A", 1, 1),
+    ("xq", "V", 2),
+    ("m1", "T", 3, 0),
+    ("ex", "A", 2, 0),
+    ("ex", "A", 2, 1),
+    ("m1", "T", 3, 1),
+    ("ex", "A", 3, 0),
+    ("C", "V", 0),
+    ("xe", "A", 3),
+    ("m1", "T", 4, 0),
+    ("ex", "A", 3, 1),
+    ("m1", "T", 4, 1),
+    ("m1", "T", 5, 0),
+    ("m1", "T", 5, 1),
+    ("C", "V", 1),
+    ("ex", "A", 4, 0),
+    ("C", "V", 2),
+    ("ex", "A", 4, 1),
+    ("xq", "V", 3),
+    ("C", "V", 3),
+    ("ex", "A", 5, 0),
+    ("m1", "T", 6, 0),
+    ("m1", "T", 6, 1),
+    ("ex", "A", 5, 1),
+    ("ex", "A", 6, 0),
+    ("a", "P", 0),
+    ("ex", "A", 6, 1),
+    ("C", "V", 4),
+    ("m1", "T", 7, 0),
+    ("C", "V", 5),
+    ("C", "V", 6),
+    ("ex", "A", 7, 0),
+    ("m1", "T", 7, 1),
+    ("dg", "P", 0),
+    ("zi", "A", 1, 1),
+    ("wo", "T", 0, 0, 0),
+    ("zw", "V", 0, 4),
+    ("wo", "T", 0, 0, 1),
+    ("ex", "A", 7, 1),
+    ("zw", "A", 1, 3),
+    ("zi", "A", 1, 2),
+    ("zw", "A", 0, 5),
+    ("zi", "A", 1, 3),
+    ("zw", "V", 1, 4),
+    ("C", "V", 7),
+    ("D", "V", 0, 0, 0),
+    ("D", "V", 0, 0, 1),
+    ("dg", "P", 1),
+    ("zw", "A", 1, 5),
+    ("zi", "A", 0, 3),
+    ("wo", "T", 0, 0, 2),
+    ("wo", "T", 0, 0, 3),
+    ("D", "V", 0, 0, 2),
+    ("D", "V", 0, 0, 3),
+    ("a", "P", 1),
+    ("zi", "A", 0, 4),
+    ("ri", "A", 0, 0),
+    ("wo", "T", 0, 1, 0),
+    ("wo", "T", 0, 1, 1),
+    ("D", "V", 0, 1, 0),
+    ("wo", "T", 0, 1, 2),
+    ("wo", "T", 0, 1, 3),
+    ("D", "V", 0, 1, 1),
+    ("D", "V", 0, 1, 2),
+    ("D", "V", 0, 1, 3),
+    ("wo", "T", 1, 0, 0),
+    ("ri", "A", 1, 0),
+    ("wo", "T", 1, 0, 1),
+    ("ri", "A", 0, 1),
+    ("D", "V", 1, 0, 0),
+    ("zq", "V", 1, 1),
+    ("wo", "T", 1, 0, 2),
+    ("wo", "T", 1, 0, 3),
+    ("D", "V", 1, 0, 1),
+    ("D", "V", 1, 0, 2),
+    ("D", "V", 1, 0, 3),
+    ("wo", "T", 1, 1, 0),
+    ("rq", "V", 0, 0),
+    ("ri", "A", 1, 1),
+    ("ri", "A", 2, 0),
+    ("m2", "T", 0, 0, 0),
+    ("zq", "V", 1, 2),
+    ("wo", "T", 1, 1, 1),
+    ("D", "V", 1, 1, 0),
+    ("wo", "T", 1, 1, 2),
+    ("rq", "V", 0, 1),
+    ("ri", "A", 3, 0),
+    ("D", "V", 1, 1, 1),
+    ("wo", "T", 1, 1, 3),
+    ("m2", "T", 1, 0, 0),
+    ("m2", "T", 0, 0, 1),
+    ("D", "V", 1, 1, 2),
+    ("m2", "T", 1, 0, 1),
+    ("m2", "T", 2, 0, 0),
+    ("D", "V", 1, 1, 3),
+    ("zi", "V", 1, 4),
+    ("zq", "V", 0, 3),
+    ("ev", "A", 0, 0),
+    ("m2", "T", 3, 0, 0),
+    ("ri", "A", 2, 1),
+    ("rq", "V", 1, 0),
+    ("m2", "T", 0, 1, 0),
+    ("m2", "T", 2, 0, 1),
+    ("m2", "T", 1, 1, 0),
+    ("ri", "V", 3, 1),
+    ("ev", "A", 1, 0),
+    ("zq", "V", 1, 3),
+    ("zq", "V", 0, 4),
+    ("m2", "T", 3, 0, 1),
+    ("rq", "V", 1, 1),
+    ("ev", "A", 2, 0),
+    ("m2", "T", 2, 1, 0),
+    ("zw", "V", 1, 6),
+    ("m2", "T", 0, 1, 1),
+    ("ev", "A", 3, 0),
+    ("ev", "A", 0, 1),
+    ("zi", "V", 0, 5),
+    ("zw", "V", 0, 6),
+    ("m2", "T", 1, 1, 1),
+    ("ev", "V", 1, 1),
+    ("m2", "T", 2, 1, 1),
+    ("zi", "V", 0, 6),
+    ("m2", "T", 3, 1, 0),
+    ("zq", "V", 1, 4),
+    ("m2", "T", 3, 1, 1),
+    ("zq", "V", 0, 5),
+    ("zi", "V", 1, 5),
+    ("m2", "T", 4, 1, 0),
+    ("m2", "T", 4, 0, 0),
+    ("zw", "V", 0, 7),
+    ("m2", "T", 4, 1, 1),
+    ("m2", "T", 4, 0, 1),
+    ("m2", "T", 5, 1, 0),
+    ("ev", "A", 2, 1),
+    ("ev", "A", 3, 1),
+    ("zq", "V", 0, 6),
+    ("ev", "A", 4, 1),
+    ("m2", "T", 5, 0, 0),
+    ("zq", "V", 1, 5),
+    ("m2", "T", 5, 1, 1),
+    ("zi", "V", 1, 6),
+    ("ev", "A", 4, 0),
+    ("m2", "T", 6, 0, 0),
+    ("ev", "A", 5, 1),
+    ("zw", "V", 1, 7),
+    ("m2", "T", 5, 0, 1),
+    ("zi", "V", 0, 7),
+    ("zq", "V", 1, 6),
+    ("zi", "A", 1, 7),
+    ("ev", "V", 5, 0),
+    ("zq", "V", 0, 7),
+    ("m2", "T", 6, 1, 0),
+    ("m2", "T", 6, 0, 1),
+    ("ev", "A", 6, 0),
+    ("m2", "T", 6, 1, 1),
+    ("zq", "V", 1, 7),
+    ("m2", "T", 7, 1, 0),
+    ("m2", "T", 7, 1, 1),
+    ("ev", "V", 6, 1),
+    ("m2", "T", 7, 0, 0),
+    ("ev", "A", 7, 1),
+    ("m2", "T", 7, 0, 1),
+    ("ev", "A", 7, 0),
+]
+
+
+def tile_choosiowhalfsweepinstrumentmoments_d1p_kernel(
+    tc, x, beta_words, beta_scales, bs, mass, obs, wt, z_bytes, z_scale, out
+):
+    nc = tc.nc
+    with ExitStack() as ctx:
+        ctx.enter_context(tc.manual_schedule())
+        sb = ctx.enter_context(tc.tile_pool(name="sb", bufs=1))
+        ps = ctx.enter_context(tc.psum_pool(name="ps", bufs=1))
+
+        def sbuf(name, shape, dtype):
+            return sb.tile(shape, dtype, name=name, align_bytes=64)
+
+        def bank(index, name, shape, dtype):
+            return ps.tile(shape, dtype, name=name, tag="bank%d" % index)
+
+        w_scales = sbuf("w_scales", [P, M], U8)
+        bs_row = sbuf("bs_row", [P, M], BF16)
+        ones = sbuf("ones", [P, P], BF16)
+        halves = sbuf("halves", [P, T], F32)
+        warm = sbuf("warm", [P, 1], F32)
+        ident = sbuf("ident", [P, P], F32)
+        nc.vector.memset(w_scales[:].bitcast(I32), 0)
+        nc.vector.memset(bs_row[:].bitcast(I32), 0)
+        nc.vector.memset(ones[:], 1.0)
+        nc.vector.memset(halves[:], 0.5)
+
+        zs = sbuf("zs", [P, G, T * 8], F32)
+        zb = {}
+        xs = {}
+        ob = {}
+        w_words = sbuf("w_words", [P, 2 * M], U8)
+        mass_sb = sbuf("mass_sb", [P, G, T], BF16)
+        wt_sb = sbuf("wt_sb", [P, G, T], BF16)
+        z_view = z_bytes.rearrange("(g p t) l -> g p t l", p=P, t=T)
+        x_view = x.rearrange("(g p t) k -> g p (t k)", p=P, t=T)
+        obs_view = obs.rearrange("(g p t) m -> g p (t m)", p=P, t=T)
+
+        def load_z(g, h):
+            zb[g, h] = sbuf("zb%d%d" % (g, h), [P, T, HALF], U8)
+            nc.sync.dma_start(out=zb[g, h][:], in_=z_view[g][:, :, h * HALF : (h + 1) * HALF])
+
+        def load_x(g):
+            xs[g] = sbuf("xs%d" % g, [P, T * K], BF16)
+            nc.sync.dma_start(out=xs[g][:], in_=x_view[g])
+
+        def load_obs(g):
+            ob[g] = sbuf("ob%d" % g, [P, T * M], BF16)
+            nc.sync.dma_start(out=ob[g][:], in_=obs_view[g])
+
+        nc.sync.dma_start(out=zs[:], in_=z_scale.rearrange("(g p t) j -> p g (t j)", p=P, t=T))
+        load_z(0, 0)
+        load_x(0)
+        nc.sync.dma_start(out=w_words[:].bitcast(I32), in_=beta_words[0].bitcast(I32))
+        for q in range(4):
+            nc.scalar.dma_start(
+                out=w_scales[32 * q : 32 * q + 4, :].bitcast(I32),
+                in_=beta_scales[0, 4 * q : 4 * q + 4, :].bitcast(I32),
+            )
+        nc.scalar.activation(out=warm[:], in_=halves[:, 0:1], func=ACT.Exp)
+        make_identity(nc, ident[:])
+        nc.gpsimd.dma_start(out=bs_row[0:1, :], in_=bs.rearrange("(o m) -> o m", o=1))
+        nc.gpsimd.dma_start(out=wt_sb[:], in_=wt.rearrange("(g p t) -> p g t", p=P, t=T))
+        nc.gpsimd.dma_start(out=mass_sb[:], in_=mass.rearrange("(g p t) -> p g t", p=P, t=T))
+        load_z(1, 0)
+        load_x(1)
+        load_obs(0)
+        load_obs(1)
+        load_z(0, 1)
+        load_z(1, 1)
+        wt_big = sbuf("wt_big", [P, G, T], F32)
+        nc.gpsimd.tensor_scalar(
+            out=wt_big[:], in0=wt_sb[:], scalar1=2048.0, scalar2=0.0, op0=ALU.mult, op1=ALU.add
+        )
+
+        t = {}
+        count = {"wo": 0, "acc": 0}
+        WO_BANKS = (7, 1, 2)
+        ACC_BANKS = (3, 4, 5, 6, 0)
+
+        def copy(eng, out_ap, in_ap):
+            if eng == "A":
+                nc.scalar.copy(out=out_ap, in_=in_ap)
+            elif eng == "P":
+                nc.gpsimd.tensor_scalar(out=out_ap, in0=in_ap, scalar1=1.0, scalar2=0.0, op0=ALU.mult, op1=ALU.add)
+            else:
+                nc.vector.tensor_copy(out=out_ap, in_=in_ap)
+
+        def interleave(eng, dst, src):
+            copy(eng, dst, src.rearrange("p t c -> p c t"))
+
+        def zw(eng, g, j):
+            wide = sbuf("zw%d%d" % (g, j), [P, T, P], BF16)
+            t["zw", g, j] = wide
+            c0 = (j % 4) * P
+            for s in range(T):
+                src = zb[g, j // 4][:, s, c0 : c0 + P].bitcast(FP8)
+                scale = zs[:, g, 8 * s + j : 8 * s + j + 1]
+                if eng == "A":
+                    nc.scalar.activation(out=wide[:, s, :], in_=src, func=ACT.Copy, scale=scale)
+                else:
+                    nc.vector.tensor_scalar(out=wide[:, s, :], in0=src, scalar1=scale, scalar2=None, op0=ALU.mult)
+
+        def zi(eng, g, j):
+            grouped = sbuf("zi%d%d" % (g, j), [P, P, T], BF16)
+            t["zi", g, j] = grouped
+            interleave(eng, grouped[:], t["zw", g, j][:])
+
+        def quantize(key, grouped, width):
+            codes = sbuf("c" + key, [P, width], U32)
+            scales = sbuf("s" + key, [P, width], U8)
+            nc.vector.quantize_mx(out=codes[:].bitcast(FP8X4), scales=scales[:], in_=grouped)
+            return codes, scales
+
+        def zq(eng, g, j):
+            t["zq", g, j] = quantize("z%d%d" % (g, j), t["zi", g, j][:].rearrange("p c t -> p (c t)"), P)
+
+        def xt(eng, b):
+            turned = bank(1 + b % 2, "xt%d" % b, [P, 2, 2, P], F32)
+            t["xt", b] = turned
+            words = xs[b // 2][:].bitcast(F32)
+            for a in range(2):
+                w0 = 256 * (2 * (b % 2) + a)
+                for u in range(2):
+                    nc.tensor.transpose(turned[:, a, u, :], words[:, w0 + u : w0 + 256 : 2], ident[:])
+
+        def xe(eng, b):
+            grouped = sbuf("xe%d" % b, [P, 2 * P * T], BF16)
+            t["xe", b] = grouped
+            copy(
+                eng,
+                grouped[:].bitcast(F32).rearrange("p (a r u) -> p a r u", a=2, u=2),
+                t["xt", b][:].rearrange("p a u r -> p a r u"),
+            )
+
+        def xq(eng, b):
+            t["xq", b] = quantize("x%d" % b, t["xe", b][:], 2 * P)
+
+        def bsb(eng):
+            spread = bank(0, "bs_spread", [P, M], BF16)
+            t["bs"] = spread
+            for h in range(2):
+                cols = slice(h * HALF, (h + 1) * HALF)
+                nc.tensor.matmul(spread[:, cols], lhsT=ones[:], rhs=bs_row[:, cols], start=True, stop=True)
+
+        def m1(eng, s, h):
+            phi = bank(3 + (2 * s + h) % 4, "phi%d%d" % (s, h), [P, HALF], F32)
+            t["phi", s, h] = phi
+            codes, scales = t["xq", s // 2]
+            cols = slice((s % 2) * P, (s % 2 + 1) * P)
+            nc.tensor.matmul_mx(
+                out=phi[:],
+                lhsT=codes[:, cols].bitcast(FP8X4),
+                lhsT_scale=scales[:, cols],
+                rhs=w_words[:, 2 * h * HALF : 2 * (h + 1) * HALF].bitcast(FP4X4),
+                rhs_scale=w_scales[:, h * HALF : (h + 1) * HALF],
+                start=True,
+                stop=True,
+            )
+
+        def ex(eng, s, h):
+            if h == 0:
+                t["E", s] = sbuf("E%d" % s, [P, M], F32)
+            nc.scalar.activation(
+                out=t["E", s][:, h * HALF : (h + 1) * HALF], in_=t["phi", s, h][:], func=ACT.Exp, scale=0.5
+            )
+
+        def cc(eng, s):
+            if s % T == 0:
+                t["hs", s // T] = sbuf("hs%d" % (s // T), [P, T], F32)
+            t["e", s] = sbuf("e%d" % s, [P, M], F32)
+            nc.vector.scalar_tensor_tensor(
+                out=t["e", s][:],
+                in0=t["E", s][:],
+                scalar=1.0 / 2048.0,
+                in1=t["bs"][:],
+                op0=ALU.mult,
+                op1=ALU.mult,
+                accum_out=t["hs", s // T][:, s % T : s % T + 1],
+            )
+
+        def aa(eng, g):
+            hs = t["hs", g]
+            sq = sbuf("sq%d" % g, [P, T], F32)
+            y = sbuf("y%d" % g, [P, T], F32)
+            root = sbuf("root%d" % g, [P, T], F32)
+            nega = sbuf("nega%d" % g, [P, T], F32)
+            coef = sbuf("coef%d" % g, [P, T], F32)
+            t["coef", g] = coef
+            nc.gpsimd.tensor_tensor(out=sq[:], in0=hs[:], in1=hs[:], op=ALU.mult)
+            nc.gpsimd.tensor_tensor(out=y[:], in0=sq[:], in1=mass_sb[:, g, :], op=ALU.add)
+            nc.gpsimd.tensor_tensor(out=root[:], in0=y[:], in1=halves[:], op=ALU.pow)
+            nc.gpsimd.tensor_tensor(out=nega[:], in0=hs[:], in1=root[:], op=ALU.subtract)
+            nc.gpsimd.tensor_tensor(out=coef[:], in0=nega[:], in1=wt_big[:, g, :], op=ALU.mult)
+
+        def dg(eng, g):
+            diag = sbuf("diag%d" % g, [P, T, P], BF16)
+            t["dg", g] = diag
+            nc.gpsimd.tensor_tensor(
+                out=diag[:],
+                in0=ident[:].unsqueeze(1).to_broadcast([P, T, P]),
+                in1=wt_sb[:, g, :].unsqueeze(2).to_broadcast([P, T, P]),
+                op=ALU.mult,
+            )
+
+        def wo(eng, h, g, s):
+            prod = bank(WO_BANKS[count["wo"] % 3], "wo%d%d%d" % (h, g, s), [P, HALF], F32)
+            count["wo"] += 1
+            t["wo", h, g, s] = prod
+            c0 = s * M + h * HALF
+            nc.tensor.matmul(prod[:], lhsT=t["dg", g][:, s, :], rhs=ob[g][:, c0 : c0 + HALF], start=True, stop=True)
+
+        def dd(eng, h, g, s):
+            if ("res", h, g) not in t:
+                t["res", h, g] = sbuf("res%d%d" % (h, g), [P, T, HALF], BF16)
+            nc.vector.scalar_tensor_tensor(
+                out=t["res", h, g][:, s, :],
+                in0=t["e", T * g + s][:, h * HALF : (h + 1) * HALF],
+                scalar=t["coef", g][:, s : s + 1],
+                in1=t["wo", h, g, s][:],
+                op0=ALU.mult,
+                op1=ALU.add,
+            )
+
+        def ri(eng, q, g):
+            h = q // 2
+            if ("ri", h, g) not in t:
+                t["ri", h, g] = sbuf("ri%d%d" % (h, g), [P, HALF, T], BF16)
+            cols = slice((q % 2) * QUART, (q % 2 + 1) * QUART)
+            interleave(eng, t["ri", h, g][:, cols, :], t["res", h, g][:, :, cols])
+
+        def rq(eng, h, g):
+            t["rq", h, g] = quantize("r%d%d" % (h, g), t["ri", h, g][:].rearrange("p c t -> p (c t)"), HALF)
+
+        def m2(eng, j, h, g):
+            if g == 0:
+                t["acc", j, h] = bank(ACC_BANKS[count["acc"] % 5], "acc%d%d" % (j, h), [P, HALF], F32)
+                count["acc"] += 1
+            z_codes, z_scales = t["zq", g, j]
+            r_codes, r_scales = t["rq", h, g]
+            nc.tensor.matmul_mx(
+                out=t["acc", j, h][:],
+                lhsT=z_codes[:].bitcast(FP8X4),
+                lhsT_scale=z_scales[:],
+                rhs=r_codes[:].bitcast(FP8X4),
+                rhs_scale=r_scales[:],
+                start=(g == 0),
+                stop=(g == G - 1),
+            )
+
+        def ev(eng, j, h):
+            result = sbuf("out%d%d" % (j, h), [P, HALF], F32)
+            copy(eng, result[:], t["acc", j, h][:])
+            nc.sync.dma_start(out=out[j * P : (j + 1) * P, h * HALF : (h + 1) * HALF], in_=result[:])
+
+        steps = {
+            "zw": zw, "zi": zi, "zq": zq, "xt": xt, "xe": xe, "xq": xq, "bs": bsb, "m1": m1, "ex": ex,
+            "C": cc, "a": aa, "dg": dg, "wo": wo, "D": dd, "ri": ri, "rq": rq, "m2": m2, "ev": ev,
+        }
+        for step in PLAN:
+            steps[step[0]](*step[1:])

@@ -24,204 +24,180 @@ HALF = 512
 QUART = 256
 
 PLAN = [
+    ("dg", "V", 0),
     ("xt", "T", 0),
-    ("zw", "A", 0, 0),
-    ("zw", "V", 0, 1),
-    ("zi", "V", 0, 0),
-    ("zw", "A", 0, 2),
-    ("zi", "V", 0, 1),
-    ("xt", "T", 1),
-    ("zw", "V", 0, 3),
     ("xe", "A", 0),
-    ("zi", "V", 0, 2),
+    ("dg", "V", 1),
     ("zw", "V", 1, 0),
     ("xq", "V", 0),
-    ("zi", "V", 1, 0),
-    ("bs", "T"),
-    ("m1", "T", 0, 0),
-    ("xt", "T", 2),
     ("zw", "V", 1, 1),
-    ("xe", "A", 1),
-    ("xq", "V", 1),
+    ("xt", "T", 1),
+    ("m1", "T", 0, 0),
     ("zw", "A", 1, 2),
-    ("ex", "A", 0, 0),
+    ("bs", "T"),
     ("m1", "T", 0, 1),
-    ("ex", "A", 0, 1),
-    ("zq", "V", 0, 0),
     ("m1", "T", 1, 0),
-    ("zq", "V", 0, 1),
-    ("xe", "V", 2),
-    ("zq", "V", 0, 2),
+    ("xe", "A", 1),
+    ("zi", "V", 1, 0),
+    ("zw", "V", 0, 0),
+    ("ex", "A", 0, 0),
     ("m1", "T", 1, 1),
+    ("xt", "T", 2),
+    ("ex", "A", 0, 1),
+    ("xq", "V", 1),
     ("m1", "T", 2, 0),
     ("ex", "A", 1, 0),
-    ("zq", "V", 1, 0),
-    ("xt", "T", 3),
+    ("C", "V", 0),
     ("m1", "T", 2, 1),
     ("ex", "A", 1, 1),
+    ("xt", "T", 3),
+    ("C", "V", 1),
+    ("zw", "V", 0, 1),
+    ("xe", "A", 2),
     ("xq", "V", 2),
     ("m1", "T", 3, 0),
     ("ex", "A", 2, 0),
-    ("ex", "A", 2, 1),
-    ("m1", "T", 3, 1),
-    ("ex", "A", 3, 0),
-    ("C", "V", 0),
     ("xe", "A", 3),
+    ("m1", "T", 3, 1),
+    ("ex", "A", 2, 1),
+    ("zi", "P", 0, 0),
+    ("xq", "V", 3),
+    ("ex", "A", 3, 0),
     ("m1", "T", 4, 0),
     ("ex", "A", 3, 1),
+    ("ex", "A", 4, 0),
     ("m1", "T", 4, 1),
     ("m1", "T", 5, 0),
-    ("m1", "T", 5, 1),
-    ("C", "V", 1),
-    ("ex", "A", 4, 0),
     ("C", "V", 2),
     ("ex", "A", 4, 1),
-    ("xq", "V", 3),
-    ("C", "V", 3),
+    ("zi", "P", 0, 1),
     ("ex", "A", 5, 0),
+    ("wo", "T", 0, 0, 0),
+    ("C", "V", 3),
+    ("C", "V", 4),
+    ("m1", "T", 5, 1),
+    ("ex", "A", 5, 1),
     ("m1", "T", 6, 0),
     ("m1", "T", 6, 1),
-    ("ex", "A", 5, 1),
-    ("ex", "A", 6, 0),
-    ("a", "P", 0),
-    ("ex", "A", 6, 1),
-    ("C", "V", 4),
-    ("m1", "T", 7, 0),
     ("C", "V", 5),
+    ("a", "P", 0),
+    ("wo", "T", 0, 0, 1),
+    ("m1", "T", 7, 0),
+    ("ex", "A", 6, 0),
+    ("ex", "A", 6, 1),
+    ("m1", "T", 7, 1),
     ("C", "V", 6),
     ("ex", "A", 7, 0),
-    ("m1", "T", 7, 1),
-    ("dg", "P", 0),
-    ("zi", "A", 1, 1),
-    ("wo", "T", 0, 0, 0),
-    ("zw", "V", 0, 4),
-    ("wo", "T", 0, 0, 1),
     ("ex", "A", 7, 1),
-    ("zw", "A", 1, 3),
-    ("zi", "A", 1, 2),
-    ("zw", "A", 0, 5),
-    ("zi", "A", 1, 3),
-    ("zw", "V", 1, 4),
     ("C", "V", 7),
+    ("zi", "P", 1, 1),
+    ("zq", "V", 0, 0),
+    ("zq", "V", 0, 1),
+    ("a", "P", 1),
     ("D", "V", 0, 0, 0),
-    ("D", "V", 0, 0, 1),
-    ("dg", "P", 1),
-    ("zw", "A", 1, 5),
-    ("zi", "A", 0, 3),
     ("wo", "T", 0, 0, 2),
     ("wo", "T", 0, 0, 3),
+    ("D", "V", 0, 0, 1),
     ("D", "V", 0, 0, 2),
+    ("zw", "A", 0, 2),
     ("D", "V", 0, 0, 3),
-    ("a", "P", 1),
-    ("zi", "A", 0, 4),
-    ("ri", "A", 0, 0),
+    ("zw", "A", 0, 3),
     ("wo", "T", 0, 1, 0),
-    ("wo", "T", 0, 1, 1),
+    ("zq", "V", 1, 0),
     ("D", "V", 0, 1, 0),
+    ("zi", "P", 1, 2),
+    ("wo", "T", 0, 1, 1),
+    ("D", "V", 0, 1, 1),
     ("wo", "T", 0, 1, 2),
     ("wo", "T", 0, 1, 3),
-    ("D", "V", 0, 1, 1),
+    ("zw", "A", 1, 3),
     ("D", "V", 0, 1, 2),
     ("D", "V", 0, 1, 3),
     ("wo", "T", 1, 0, 0),
-    ("ri", "A", 1, 0),
-    ("wo", "T", 1, 0, 1),
-    ("ri", "A", 0, 1),
     ("D", "V", 1, 0, 0),
-    ("zq", "V", 1, 1),
-    ("wo", "T", 1, 0, 2),
-    ("wo", "T", 1, 0, 3),
+    ("zi", "A", 0, 2),
+    ("ri", "A", 0, 0, 0),
+    ("ri", "A", 0, 0, 1),
+    ("ri", "A", 0, 1, 0),
+    ("wo", "T", 1, 0, 1),
+    ("ri", "A", 0, 1, 1),
     ("D", "V", 1, 0, 1),
-    ("D", "V", 1, 0, 2),
-    ("D", "V", 1, 0, 3),
-    ("wo", "T", 1, 1, 0),
     ("rq", "V", 0, 0),
-    ("ri", "A", 1, 1),
-    ("ri", "A", 2, 0),
-    ("m2", "T", 0, 0, 0),
-    ("zq", "V", 1, 2),
+    ("wo", "T", 1, 1, 0),
+    ("ri", "A", 1, 0, 0),
     ("wo", "T", 1, 1, 1),
+    ("m2", "T", 0, 0, 0),
     ("D", "V", 1, 1, 0),
-    ("wo", "T", 1, 1, 2),
-    ("rq", "V", 0, 1),
-    ("ri", "A", 3, 0),
-    ("D", "V", 1, 1, 1),
-    ("wo", "T", 1, 1, 3),
-    ("m2", "T", 1, 0, 0),
-    ("m2", "T", 0, 0, 1),
-    ("D", "V", 1, 1, 2),
-    ("m2", "T", 1, 0, 1),
-    ("m2", "T", 2, 0, 0),
-    ("D", "V", 1, 1, 3),
-    ("zi", "V", 1, 4),
-    ("zq", "V", 0, 3),
-    ("ev", "A", 0, 0),
-    ("m2", "T", 3, 0, 0),
-    ("ri", "A", 2, 1),
-    ("rq", "V", 1, 0),
     ("m2", "T", 0, 1, 0),
-    ("m2", "T", 2, 0, 1),
-    ("m2", "T", 1, 1, 0),
-    ("ri", "V", 3, 1),
-    ("ev", "A", 1, 0),
-    ("zq", "V", 1, 3),
-    ("zq", "V", 0, 4),
-    ("m2", "T", 3, 0, 1),
-    ("rq", "V", 1, 1),
-    ("ev", "A", 2, 0),
-    ("m2", "T", 2, 1, 0),
-    ("zw", "V", 1, 6),
+    ("wo", "T", 2, 0, 0),
+    ("wo", "T", 2, 0, 1),
+    ("D", "V", 1, 1, 1),
+    ("rq", "V", 0, 1),
+    ("m2", "T", 0, 2, 0),
+    ("wo", "T", 2, 1, 0),
+    ("m2", "T", 0, 3, 0),
+    ("zq", "V", 0, 2),
+    ("zi", "P", 0, 3),
+    ("m2", "T", 0, 0, 1),
+    ("zq", "V", 1, 1),
     ("m2", "T", 0, 1, 1),
-    ("ev", "A", 3, 0),
+    ("zi", "P", 1, 3),
+    ("ev", "V", 0, 0),
+    ("m2", "T", 0, 4, 0),
+    ("m2", "T", 0, 2, 1),
+    ("m2", "T", 0, 5, 0),
+    ("m2", "T", 0, 3, 1),
+    ("zq", "V", 0, 3),
+    ("zq", "V", 1, 2),
+    ("ri", "A", 1, 1, 0),
+    ("zq", "V", 1, 3),
     ("ev", "A", 0, 1),
-    ("zi", "V", 0, 5),
-    ("zw", "V", 0, 6),
+    ("rq", "V", 1, 0),
+    ("m2", "T", 0, 4, 1),
+    ("m2", "T", 0, 6, 0),
+    ("rq", "V", 1, 1),
+    ("m2", "T", 0, 5, 1),
+    ("ev", "A", 0, 2),
+    ("m2", "T", 0, 6, 1),
+    ("D", "V", 2, 0, 0),
+    ("m2", "T", 1, 0, 1),
+    ("wo", "T", 2, 1, 1),
+    ("D", "V", 2, 0, 1),
+    ("ev", "A", 0, 3),
+    ("ev", "A", 0, 4),
+    ("D", "V", 2, 1, 0),
+    ("ev", "A", 0, 5),
     ("m2", "T", 1, 1, 1),
-    ("ev", "V", 1, 1),
+    ("m2", "T", 0, 7, 0),
+    ("ev", "A", 0, 6),
+    ("D", "V", 2, 1, 1),
+    ("ev", "A", 1, 0),
+    ("m2", "T", 0, 7, 1),
+    ("ev", "A", 0, 7),
+    ("ri", "V", 2, 0, 0),
+    ("m2", "T", 1, 2, 1),
+    ("ri", "V", 2, 1, 0),
+    ("rq", "V", 2, 0),
+    ("ev", "A", 1, 1),
+    ("m2", "T", 1, 3, 1),
+    ("ev", "A", 1, 2),
+    ("rq", "V", 2, 1),
+    ("m2", "T", 2, 0, 1),
     ("m2", "T", 2, 1, 1),
-    ("zi", "V", 0, 6),
-    ("m2", "T", 3, 1, 0),
-    ("zq", "V", 1, 4),
-    ("m2", "T", 3, 1, 1),
-    ("zq", "V", 0, 5),
-    ("zi", "V", 1, 5),
-    ("m2", "T", 4, 1, 0),
-    ("m2", "T", 4, 0, 0),
-    ("zw", "V", 0, 7),
-    ("m2", "T", 4, 1, 1),
-    ("m2", "T", 4, 0, 1),
-    ("m2", "T", 5, 1, 0),
-    ("ev", "A", 2, 1),
-    ("ev", "A", 3, 1),
-    ("zq", "V", 0, 6),
-    ("ev", "A", 4, 1),
-    ("m2", "T", 5, 0, 0),
-    ("zq", "V", 1, 5),
-    ("m2", "T", 5, 1, 1),
-    ("zi", "V", 1, 6),
-    ("ev", "A", 4, 0),
-    ("m2", "T", 6, 0, 0),
-    ("ev", "A", 5, 1),
-    ("zw", "V", 1, 7),
-    ("m2", "T", 5, 0, 1),
-    ("zi", "V", 0, 7),
-    ("zq", "V", 1, 6),
-    ("zi", "A", 1, 7),
-    ("ev", "V", 5, 0),
-    ("zq", "V", 0, 7),
-    ("m2", "T", 6, 1, 0),
-    ("m2", "T", 6, 0, 1),
-    ("ev", "A", 6, 0),
-    ("m2", "T", 6, 1, 1),
-    ("zq", "V", 1, 7),
-    ("m2", "T", 7, 1, 0),
-    ("m2", "T", 7, 1, 1),
-    ("ev", "V", 6, 1),
-    ("m2", "T", 7, 0, 0),
-    ("ev", "A", 7, 1),
-    ("m2", "T", 7, 0, 1),
-    ("ev", "A", 7, 0),
+    ("ev", "A", 1, 3),
+    ("m2", "T", 2, 2, 1),
+    ("ev", "A", 2, 0),
+    ("m2", "T", 2, 3, 1),
+    ("ev", "V", 2, 1),
+    ("ev", "V", 2, 2),
+    ("ev", "A", 2, 3),
 ]
+
+CH = [512,256,256]
+LOADS = ["x0","zs","z1","x1","W","z0","x2","x3","o0","o1"]
+I4 = True
+START = [sum(CH[:q]) for q in range(len(CH))]
+ZW = 256
 
 
 def tile_choosiowhalfsweepinstrumentmoments_d1p_kernel(
@@ -257,26 +233,37 @@ def tile_choosiowhalfsweepinstrumentmoments_d1p_kernel(
         w_words = sbuf("w_words", [P, 2 * M], U8)
         mass_sb = sbuf("mass_sb", [P, G, T], BF16)
         wt_sb = sbuf("wt_sb", [P, G, T], BF16)
-        z_view = z_bytes.rearrange("(g p t) l -> g p t l", p=P, t=T)
+        z_view = z_bytes.rearrange("(g p t) l -> g p (t l)", p=P, t=T)
         x_view = x.rearrange("(g p t) k -> g p (t k)", p=P, t=T)
         obs_view = obs.rearrange("(g p t) m -> g p (t m)", p=P, t=T)
 
-        def load_z(g, h):
-            zb[g, h] = sbuf("zb%d%d" % (g, h), [P, T, HALF], U8)
-            nc.sync.dma_start(out=zb[g, h][:], in_=z_view[g][:, :, h * HALF : (h + 1) * HALF])
+        def load_z(g):
+            zb[g] = sbuf("zb%d" % g, [P, T * L], U8)
+            nc.sync.dma_start(out=zb[g][:], in_=z_view[g])
 
-        def load_x(g):
-            xs[g] = sbuf("xs%d" % g, [P, T * K], BF16)
-            nc.sync.dma_start(out=xs[g][:], in_=x_view[g])
+        def load_x(b):
+            xs[b] = sbuf("xs%d" % b, [P, 2 * K], BF16)
+            nc.sync.dma_start(out=xs[b][:], in_=x_view[b // 2][:, (b % 2) * 2 * K : (b % 2 + 1) * 2 * K])
 
         def load_obs(g):
             ob[g] = sbuf("ob%d" % g, [P, T * M], BF16)
             nc.sync.dma_start(out=ob[g][:], in_=obs_view[g])
 
-        nc.sync.dma_start(out=zs[:], in_=z_scale.rearrange("(g p t) j -> p g (t j)", p=P, t=T))
-        load_z(0, 0)
-        load_x(0)
-        nc.sync.dma_start(out=w_words[:].bitcast(I32), in_=beta_words[0].bitcast(I32))
+        def load(name):
+            if name == "zs":
+                nc.sync.dma_start(out=zs[:], in_=z_scale.rearrange("(g p t) j -> p g (t j)", p=P, t=T))
+            elif name == "W":
+                nc.sync.dma_start(out=w_words[:].bitcast(I32), in_=beta_words[0].bitcast(I32))
+            elif name[0] == "x":
+                load_x(int(name[1]))
+            elif name[0] == "o":
+                load_obs(int(name[1]))
+            else:
+                load_z(int(name[1]))
+
+        nc.scalar.dma_start(out=wt_sb[:], in_=wt.rearrange("(g p t) -> p g t", p=P, t=T))
+        for name in LOADS[:3]:
+            load(name)
         for q in range(4):
             nc.scalar.dma_start(
                 out=w_scales[32 * q : 32 * q + 4, :].bitcast(I32),
@@ -285,14 +272,9 @@ def tile_choosiowhalfsweepinstrumentmoments_d1p_kernel(
         nc.scalar.activation(out=warm[:], in_=halves[:, 0:1], func=ACT.Exp)
         make_identity(nc, ident[:])
         nc.gpsimd.dma_start(out=bs_row[0:1, :], in_=bs.rearrange("(o m) -> o m", o=1))
-        nc.gpsimd.dma_start(out=wt_sb[:], in_=wt.rearrange("(g p t) -> p g t", p=P, t=T))
         nc.gpsimd.dma_start(out=mass_sb[:], in_=mass.rearrange("(g p t) -> p g t", p=P, t=T))
-        load_z(1, 0)
-        load_x(1)
-        load_obs(0)
-        load_obs(1)
-        load_z(0, 1)
-        load_z(1, 1)
+        for name in LOADS[3:]:
+            load(name)
         wt_big = sbuf("wt_big", [P, G, T], F32)
         nc.gpsimd.tensor_scalar(
             out=wt_big[:], in0=wt_sb[:], scalar1=2048.0, scalar2=0.0, op0=ALU.mult, op1=ALU.add
@@ -312,24 +294,30 @@ def tile_choosiowhalfsweepinstrumentmoments_d1p_kernel(
                 nc.vector.tensor_copy(out=out_ap, in_=in_ap)
 
         def interleave(eng, dst, src):
-            copy(eng, dst, src.rearrange("p t c -> p c t"))
+            if I4 and eng != "P":
+                copy(eng, dst.rearrange("p (c i) t -> p c t i", i=4), src.rearrange("p t (c i) -> p c t i", i=4))
+            else:
+                copy(eng, dst, src.rearrange("p t c -> p c t"))
 
-        def zw(eng, g, j):
-            wide = sbuf("zw%d%d" % (g, j), [P, T, P], BF16)
-            t["zw", g, j] = wide
-            c0 = (j % 4) * P
+        def zw(eng, g, u):
+            wide = sbuf("zw%d%d" % (g, u), [P, T, ZW], BF16)
+            t["zw", g, u] = wide
             for s in range(T):
-                src = zb[g, j // 4][:, s, c0 : c0 + P].bitcast(FP8)
-                scale = zs[:, g, 8 * s + j : 8 * s + j + 1]
-                if eng == "A":
-                    nc.scalar.activation(out=wide[:, s, :], in_=src, func=ACT.Copy, scale=scale)
-                else:
-                    nc.vector.tensor_scalar(out=wide[:, s, :], in0=src, scalar1=scale, scalar2=None, op0=ALU.mult)
+                for jj in range(2):
+                    j = 2 * u + jj
+                    c0 = s * L + j * P
+                    src = zb[g][:, c0 : c0 + P].bitcast(FP8)
+                    scale = zs[:, g, 8 * s + j : 8 * s + j + 1]
+                    dst = wide[:, s, jj * P : (jj + 1) * P]
+                    if eng == "A":
+                        nc.scalar.activation(out=dst, in_=src, func=ACT.Copy, scale=scale)
+                    else:
+                        nc.vector.tensor_scalar(out=dst, in0=src, scalar1=scale, scalar2=None, op0=ALU.mult)
 
-        def zi(eng, g, j):
-            grouped = sbuf("zi%d%d" % (g, j), [P, P, T], BF16)
-            t["zi", g, j] = grouped
-            interleave(eng, grouped[:], t["zw", g, j][:])
+        def zi(eng, g, u):
+            grouped = sbuf("zi%d%d" % (g, u), [P, ZW, T], BF16)
+            t["zi", g, u] = grouped
+            interleave(eng, grouped[:], t["zw", g, u][:])
 
         def quantize(key, grouped, width):
             codes = sbuf("c" + key, [P, width], U32)
@@ -338,14 +326,14 @@ def tile_choosiowhalfsweepinstrumentmoments_d1p_kernel(
             return codes, scales
 
         def zq(eng, g, j):
-            t["zq", g, j] = quantize("z%d%d" % (g, j), t["zi", g, j][:].rearrange("p c t -> p (c t)"), P)
+            t["zq", g, j] = quantize("z%d%d" % (g, j), t["zi", g, j][:].rearrange("p c t -> p (c t)"), ZW)
 
         def xt(eng, b):
             turned = bank(1 + b % 2, "xt%d" % b, [P, 2, 2, P], F32)
             t["xt", b] = turned
-            words = xs[b // 2][:].bitcast(F32)
+            words = xs[b][:].bitcast(F32)
             for a in range(2):
-                w0 = 256 * (2 * (b % 2) + a)
+                w0 = 256 * a
                 for u in range(2):
                     nc.tensor.transpose(turned[:, a, u, :], words[:, w0 + u : w0 + 256 : 2], ident[:])
 
@@ -404,83 +392,111 @@ def tile_choosiowhalfsweepinstrumentmoments_d1p_kernel(
                 accum_out=t["hs", s // T][:, s % T : s % T + 1],
             )
 
+        def small(key, g):
+            t[key, g] = sbuf("%s%d" % (key, g), [P, T], F32)
+            return t[key, g][:]
+
+        def y1(eng, g):
+            nc.vector.tensor_tensor(out=small("sq", g), in0=t["hs", g][:], in1=t["hs", g][:], op=ALU.mult)
+
+        def y2(eng, g):
+            nc.vector.tensor_tensor(out=small("y", g), in0=t["sq", g][:], in1=mass_sb[:, g, :], op=ALU.add)
+
+        def pw(eng, g):
+            nc.gpsimd.tensor_tensor(out=small("root", g), in0=t["y", g][:], in1=halves[:], op=ALU.pow)
+
+        def c1(eng, g):
+            nc.vector.tensor_tensor(out=small("nega", g), in0=t["hs", g][:], in1=t["root", g][:], op=ALU.subtract)
+
         def aa(eng, g):
-            hs = t["hs", g]
-            sq = sbuf("sq%d" % g, [P, T], F32)
-            y = sbuf("y%d" % g, [P, T], F32)
-            root = sbuf("root%d" % g, [P, T], F32)
-            nega = sbuf("nega%d" % g, [P, T], F32)
-            coef = sbuf("coef%d" % g, [P, T], F32)
-            t["coef", g] = coef
-            nc.gpsimd.tensor_tensor(out=sq[:], in0=hs[:], in1=hs[:], op=ALU.mult)
-            nc.gpsimd.tensor_tensor(out=y[:], in0=sq[:], in1=mass_sb[:, g, :], op=ALU.add)
-            nc.gpsimd.tensor_tensor(out=root[:], in0=y[:], in1=halves[:], op=ALU.pow)
-            nc.gpsimd.tensor_tensor(out=nega[:], in0=hs[:], in1=root[:], op=ALU.subtract)
-            nc.gpsimd.tensor_tensor(out=coef[:], in0=nega[:], in1=wt_big[:, g, :], op=ALU.mult)
+            if eng == "P":
+                hs = t["hs", g]
+                nc.gpsimd.tensor_tensor(out=small("sq", g), in0=hs[:], in1=hs[:], op=ALU.mult)
+                nc.gpsimd.tensor_tensor(out=small("y", g), in0=t["sq", g][:], in1=mass_sb[:, g, :], op=ALU.add)
+                pw(eng, g)
+                nc.gpsimd.tensor_tensor(out=small("nega", g), in0=hs[:], in1=t["root", g][:], op=ALU.subtract)
+                nc.gpsimd.tensor_tensor(out=small("coef", g), in0=t["nega", g][:], in1=wt_big[:, g, :], op=ALU.mult)
+            else:
+                nc.vector.tensor_tensor(out=small("coef", g), in0=t["nega", g][:], in1=wt_big[:, g, :], op=ALU.mult)
 
         def dg(eng, g):
             diag = sbuf("diag%d" % g, [P, T, P], BF16)
             t["dg", g] = diag
-            nc.gpsimd.tensor_tensor(
-                out=diag[:],
-                in0=ident[:].unsqueeze(1).to_broadcast([P, T, P]),
-                in1=wt_sb[:, g, :].unsqueeze(2).to_broadcast([P, T, P]),
-                op=ALU.mult,
-            )
+            for s in range(T):
+                nc.vector.tensor_scalar(
+                    out=diag[:, s, :], in0=ident[:], scalar1=wt_sb[:, g, s : s + 1], scalar2=None, op0=ALU.mult
+                )
 
-        def wo(eng, h, g, s):
-            prod = bank(WO_BANKS[count["wo"] % 3], "wo%d%d%d" % (h, g, s), [P, HALF], F32)
+        def wo(eng, q, g, b):
+            w = CH[q]
+            per = HALF // w
+            prod = bank(WO_BANKS[count["wo"] % 3], "wo%d%d%d" % (q, g, b), [P, per, w], F32)
             count["wo"] += 1
-            t["wo", h, g, s] = prod
-            c0 = s * M + h * HALF
-            nc.tensor.matmul(prod[:], lhsT=t["dg", g][:, s, :], rhs=ob[g][:, c0 : c0 + HALF], start=True, stop=True)
+            t["wo", q, g, b] = prod
+            for i in range(per):
+                s = b * per + i
+                c0 = s * M + START[q]
+                nc.tensor.matmul(prod[:, i, :], lhsT=t["dg", g][:, s, :], rhs=ob[g][:, c0 : c0 + w], start=True, stop=True)
 
-        def dd(eng, h, g, s):
-            if ("res", h, g) not in t:
-                t["res", h, g] = sbuf("res%d%d" % (h, g), [P, T, HALF], BF16)
-            nc.vector.scalar_tensor_tensor(
-                out=t["res", h, g][:, s, :],
-                in0=t["e", T * g + s][:, h * HALF : (h + 1) * HALF],
-                scalar=t["coef", g][:, s : s + 1],
-                in1=t["wo", h, g, s][:],
-                op0=ALU.mult,
-                op1=ALU.add,
-            )
+        def dd(eng, q, g, b):
+            w = CH[q]
+            per = HALF // w
+            if b == 0:
+                t["res", q, g] = sbuf("res%d%d" % (q, g), [P, T, w], BF16)
+            for i in range(per):
+                s = b * per + i
+                nc.vector.scalar_tensor_tensor(
+                    out=t["res", q, g][:, s, :],
+                    in0=t["e", T * g + s][:, START[q] : START[q] + w],
+                    scalar=t["coef", g][:, s : s + 1],
+                    in1=t["wo", q, g, b][:, i, :],
+                    op0=ALU.mult,
+                    op1=ALU.add,
+                )
 
-        def ri(eng, q, g):
-            h = q // 2
-            if ("ri", h, g) not in t:
-                t["ri", h, g] = sbuf("ri%d%d" % (h, g), [P, HALF, T], BF16)
-            cols = slice((q % 2) * QUART, (q % 2 + 1) * QUART)
-            interleave(eng, t["ri", h, g][:, cols, :], t["res", h, g][:, :, cols])
+        def ri(eng, q, g, i):
+            w = CH[q]
+            if ("ri", q, g) not in t:
+                t["ri", q, g] = sbuf("ri%d%d" % (q, g), [P, w, T], BF16)
+            cols = slice(i * QUART, min(w, (i + 1) * QUART))
+            interleave(eng, t["ri", q, g][:, cols, :], t["res", q, g][:, :, cols])
 
-        def rq(eng, h, g):
-            t["rq", h, g] = quantize("r%d%d" % (h, g), t["ri", h, g][:].rearrange("p c t -> p (c t)"), HALF)
+        def rq(eng, q, g):
+            t["rq", q, g] = quantize("r%d%d" % (q, g), t["ri", q, g][:].rearrange("p c t -> p (c t)"), CH[q])
 
-        def m2(eng, j, h, g):
-            if g == 0:
-                t["acc", j, h] = bank(ACC_BANKS[count["acc"] % 5], "acc%d%d" % (j, h), [P, HALF], F32)
+        def m2(eng, q, b, g):
+            w = CH[q]
+            per = HALF // w
+            if g == 0 or per > 1:
+                t["acc", q, b] = bank(ACC_BANKS[count["acc"] % 5], "acc%d%d" % (q, b), [P, per, w], F32)
                 count["acc"] += 1
-            z_codes, z_scales = t["zq", g, j]
-            r_codes, r_scales = t["rq", h, g]
-            nc.tensor.matmul_mx(
-                out=t["acc", j, h][:],
-                lhsT=z_codes[:].bitcast(FP8X4),
-                lhsT_scale=z_scales[:],
-                rhs=r_codes[:].bitcast(FP8X4),
-                rhs_scale=r_scales[:],
-                start=(g == 0),
-                stop=(g == G - 1),
-            )
+            for i in range(per):
+                j = b * per + i
+                cols = slice((j % 2) * P, (j % 2 + 1) * P)
+                for gg in ([g] if per == 1 else range(G)):
+                    z_codes, z_scales = t["zq", gg, j // 2]
+                    r_codes, r_scales = t["rq", q, gg]
+                    nc.tensor.matmul_mx(
+                        out=t["acc", q, b][:, i, :],
+                        lhsT=z_codes[:, cols].bitcast(FP8X4),
+                        lhsT_scale=z_scales[:, cols],
+                        rhs=r_codes[:].bitcast(FP8X4),
+                        rhs_scale=r_scales[:],
+                        start=(gg == 0),
+                        stop=(gg == G - 1),
+                    )
 
-        def ev(eng, j, h):
-            result = sbuf("out%d%d" % (j, h), [P, HALF], F32)
-            copy(eng, result[:], t["acc", j, h][:])
-            nc.sync.dma_start(out=out[j * P : (j + 1) * P, h * HALF : (h + 1) * HALF], in_=result[:])
+        def ev(eng, q, b):
+            w = CH[q]
+            per = HALF // w
+            result = sbuf("out%d%d" % (q, b), [P, per, w], F32)
+            copy(eng, result[:], t["acc", q, b][:])
+            rows = out[b * per * P : (b + 1) * per * P, START[q] : START[q] + w]
+            nc.sync.dma_start(out=rows.rearrange("(i l) m -> l i m", l=P), in_=result[:])
 
         steps = {
             "zw": zw, "zi": zi, "zq": zq, "xt": xt, "xe": xe, "xq": xq, "bs": bsb, "m1": m1, "ex": ex,
-            "C": cc, "a": aa, "dg": dg, "wo": wo, "D": dd, "ri": ri, "rq": rq, "m2": m2, "ev": ev,
+            "C": cc, "a": aa, "y1": y1, "y2": y2, "pw": pw, "c1": c1, "dg": dg, "wo": wo, "D": dd, "ri": ri, "rq": rq, "m2": m2, "ev": ev,
         }
         for step in PLAN:
             steps[step[0]](*step[1:])

@@ -26,175 +26,175 @@ QUART = 256
 PLAN = [
     ("dg", "V", 0),
     ("xt", "T", 0),
-    ("xe", "A", 0),
     ("dg", "V", 1),
     ("zw", "V", 1, 0),
-    ("xq", "V", 0),
-    ("zw", "V", 1, 1),
-    ("xt", "T", 1),
-    ("m1", "T", 0, 0),
-    ("zw", "A", 1, 2),
     ("bs", "T"),
+    ("xe", "A", 0),
+    ("xq", "V", 0),
+    ("xt", "T", 1),
+    ("zw", "A", 1, 2),
+    ("m1", "T", 0, 0),
+    ("zw", "V", 1, 3),
     ("m1", "T", 0, 1),
-    ("m1", "T", 1, 0),
+    ("zw", "V", 1, 1),
     ("xe", "A", 1),
-    ("zi", "V", 1, 0),
-    ("zw", "V", 0, 0),
     ("ex", "A", 0, 0),
+    ("m1", "T", 1, 0),
     ("m1", "T", 1, 1),
-    ("xt", "T", 2),
-    ("ex", "A", 0, 1),
+    ("zw", "V", 0, 0),
     ("xq", "V", 1),
-    ("m1", "T", 2, 0),
-    ("ex", "A", 1, 0),
+    ("ex", "A", 0, 1),
     ("C", "V", 0),
-    ("m1", "T", 2, 1),
+    ("xt", "T", 2),
+    ("m1", "T", 2, 0),
+    ("zi", "P", 0, 0),
+    ("ex", "A", 1, 0),
     ("ex", "A", 1, 1),
     ("xt", "T", 3),
-    ("C", "V", 1),
-    ("zw", "V", 0, 1),
     ("xe", "A", 2),
-    ("xq", "V", 2),
-    ("m1", "T", 3, 0),
-    ("ex", "A", 2, 0),
+    ("C", "V", 1),
+    ("m1", "T", 2, 1),
     ("xe", "A", 3),
-    ("m1", "T", 3, 1),
+    ("xq", "V", 2),
+    ("ex", "A", 2, 0),
+    ("m1", "T", 3, 0),
     ("ex", "A", 2, 1),
-    ("zi", "P", 0, 0),
-    ("xq", "V", 3),
     ("ex", "A", 3, 0),
+    ("m1", "T", 3, 1),
+    ("zw", "V", 0, 1),
+    ("xq", "V", 3),
     ("m1", "T", 4, 0),
-    ("ex", "A", 3, 1),
-    ("ex", "A", 4, 0),
     ("m1", "T", 4, 1),
     ("m1", "T", 5, 0),
-    ("C", "V", 2),
+    ("ex", "A", 3, 1),
+    ("wo", "T", 0, 0, 0),
+    ("ex", "A", 4, 0),
     ("ex", "A", 4, 1),
     ("zi", "P", 0, 1),
-    ("ex", "A", 5, 0),
-    ("wo", "T", 0, 0, 0),
-    ("C", "V", 3),
-    ("C", "V", 4),
     ("m1", "T", 5, 1),
+    ("ex", "A", 5, 0),
     ("ex", "A", 5, 1),
+    ("zi", "P", 1, 0),
+    ("C", "V", 2),
     ("m1", "T", 6, 0),
-    ("m1", "T", 6, 1),
-    ("C", "V", 5),
-    ("a", "P", 0),
-    ("wo", "T", 0, 0, 1),
-    ("m1", "T", 7, 0),
     ("ex", "A", 6, 0),
+    ("m1", "T", 6, 1),
+    ("C", "V", 3),
+    ("wo", "T", 0, 0, 1),
     ("ex", "A", 6, 1),
+    ("m1", "T", 7, 0),
     ("m1", "T", 7, 1),
-    ("C", "V", 6),
+    ("C", "V", 4),
+    ("wo", "T", 0, 0, 2),
+    ("a", "P", 0),
     ("ex", "A", 7, 0),
     ("ex", "A", 7, 1),
+    ("zw", "A", 0, 2),
+    ("C", "V", 5),
+    ("C", "V", 6),
     ("C", "V", 7),
-    ("zi", "P", 1, 1),
-    ("zq", "V", 0, 0),
-    ("zq", "V", 0, 1),
     ("a", "P", 1),
+    ("zq", "V", 0, 0),
     ("D", "V", 0, 0, 0),
-    ("wo", "T", 0, 0, 2),
+    ("zi", "A", 1, 2),
     ("wo", "T", 0, 0, 3),
     ("D", "V", 0, 0, 1),
-    ("D", "V", 0, 0, 2),
-    ("zw", "A", 0, 2),
-    ("D", "V", 0, 0, 3),
     ("zw", "A", 0, 3),
     ("wo", "T", 0, 1, 0),
-    ("zq", "V", 1, 0),
-    ("D", "V", 0, 1, 0),
-    ("zi", "P", 1, 2),
+    ("D", "V", 0, 0, 2),
+    ("zi", "A", 1, 1),
     ("wo", "T", 0, 1, 1),
+    ("D", "V", 0, 0, 3),
+    ("D", "V", 0, 1, 0),
     ("D", "V", 0, 1, 1),
     ("wo", "T", 0, 1, 2),
     ("wo", "T", 0, 1, 3),
-    ("zw", "A", 1, 3),
-    ("D", "V", 0, 1, 2),
-    ("D", "V", 0, 1, 3),
-    ("wo", "T", 1, 0, 0),
-    ("D", "V", 1, 0, 0),
-    ("zi", "A", 0, 2),
     ("ri", "A", 0, 0, 0),
-    ("ri", "A", 0, 0, 1),
-    ("ri", "A", 0, 1, 0),
+    ("D", "V", 0, 1, 2),
+    ("wo", "T", 1, 0, 0),
     ("wo", "T", 1, 0, 1),
-    ("ri", "A", 0, 1, 1),
+    ("D", "V", 0, 1, 3),
+    ("ri", "A", 0, 0, 1),
+    ("D", "V", 1, 0, 0),
+    ("zi", "P", 0, 2),
     ("D", "V", 1, 0, 1),
-    ("rq", "V", 0, 0),
     ("wo", "T", 1, 1, 0),
-    ("ri", "A", 1, 0, 0),
-    ("wo", "T", 1, 1, 1),
-    ("m2", "T", 0, 0, 0),
+    ("ri", "A", 0, 1, 0),
     ("D", "V", 1, 1, 0),
-    ("m2", "T", 0, 1, 0),
-    ("wo", "T", 2, 0, 0),
-    ("wo", "T", 2, 0, 1),
-    ("D", "V", 1, 1, 1),
-    ("rq", "V", 0, 1),
-    ("m2", "T", 0, 2, 0),
-    ("wo", "T", 2, 1, 0),
-    ("m2", "T", 0, 3, 0),
-    ("zq", "V", 0, 2),
-    ("zi", "P", 0, 3),
-    ("m2", "T", 0, 0, 1),
-    ("zq", "V", 1, 1),
-    ("m2", "T", 0, 1, 1),
+    ("ri", "A", 0, 1, 1),
     ("zi", "P", 1, 3),
-    ("ev", "V", 0, 0),
-    ("m2", "T", 0, 4, 0),
-    ("m2", "T", 0, 2, 1),
-    ("m2", "T", 0, 5, 0),
-    ("m2", "T", 0, 3, 1),
-    ("zq", "V", 0, 3),
+    ("wo", "T", 1, 1, 1),
+    ("zq", "V", 1, 0),
+    ("rq", "V", 0, 0),
+    ("m2", "T", 0, 0, 0),
+    ("wo", "T", 2, 0, 0),
+    ("zq", "V", 0, 2),
+    ("zq", "V", 0, 1),
+    ("rq", "V", 0, 1),
+    ("m2", "T", 0, 1, 0),
+    ("wo", "T", 2, 0, 1),
+    ("m2", "T", 0, 0, 1),
+    ("m2", "T", 0, 2, 0),
     ("zq", "V", 1, 2),
-    ("ri", "A", 1, 1, 0),
+    ("zq", "V", 1, 1),
+    ("zi", "A", 0, 3),
+    ("D", "V", 1, 1, 1),
     ("zq", "V", 1, 3),
-    ("ev", "A", 0, 1),
+    ("ri", "A", 1, 0, 0),
+    ("ev", "A", 0, 0),
     ("rq", "V", 1, 0),
-    ("m2", "T", 0, 4, 1),
-    ("m2", "T", 0, 6, 0),
-    ("rq", "V", 1, 1),
-    ("m2", "T", 0, 5, 1),
+    ("m2", "T", 0, 1, 1),
+    ("m2", "T", 0, 3, 0),
+    ("m2", "T", 0, 2, 1),
+    ("ri", "V", 1, 1, 0),
+    ("ev", "A", 0, 1),
+    ("m2", "T", 0, 4, 0),
+    ("m2", "T", 0, 3, 1),
+    ("m2", "T", 0, 5, 0),
     ("ev", "A", 0, 2),
-    ("m2", "T", 0, 6, 1),
-    ("D", "V", 2, 0, 0),
-    ("m2", "T", 1, 0, 1),
-    ("wo", "T", 2, 1, 1),
-    ("D", "V", 2, 0, 1),
     ("ev", "A", 0, 3),
-    ("ev", "A", 0, 4),
+    ("D", "V", 2, 0, 0),
+    ("wo", "T", 2, 1, 0),
+    ("rq", "V", 1, 1),
+    ("m2", "T", 0, 4, 1),
+    ("D", "V", 2, 0, 1),
+    ("zq", "V", 0, 3),
     ("D", "V", 2, 1, 0),
-    ("ev", "A", 0, 5),
-    ("m2", "T", 1, 1, 1),
-    ("m2", "T", 0, 7, 0),
-    ("ev", "A", 0, 6),
+    ("m2", "T", 0, 5, 1),
+    ("wo", "T", 2, 1, 1),
     ("D", "V", 2, 1, 1),
-    ("ev", "A", 1, 0),
-    ("m2", "T", 0, 7, 1),
-    ("ev", "A", 0, 7),
     ("ri", "V", 2, 0, 0),
-    ("m2", "T", 1, 2, 1),
+    ("ev", "A", 0, 4),
+    ("m2", "T", 1, 0, 1),
+    ("m2", "T", 1, 1, 1),
     ("ri", "V", 2, 1, 0),
+    ("ev", "A", 0, 5),
+    ("m2", "T", 0, 6, 0),
+    ("m2", "T", 0, 6, 1),
     ("rq", "V", 2, 0),
-    ("ev", "A", 1, 1),
-    ("m2", "T", 1, 3, 1),
-    ("ev", "A", 1, 2),
+    ("ev", "A", 1, 0),
     ("rq", "V", 2, 1),
+    ("m2", "T", 0, 7, 0),
+    ("ev", "A", 1, 1),
+    ("m2", "T", 1, 2, 1),
+    ("ev", "A", 0, 6),
+    ("ev", "A", 1, 2),
+    ("m2", "T", 0, 7, 1),
+    ("m2", "T", 1, 3, 1),
     ("m2", "T", 2, 0, 1),
-    ("m2", "T", 2, 1, 1),
     ("ev", "A", 1, 3),
-    ("m2", "T", 2, 2, 1),
+    ("ev", "V", 0, 7),
+    ("m2", "T", 2, 1, 1),
     ("ev", "A", 2, 0),
-    ("m2", "T", 2, 3, 1),
-    ("ev", "V", 2, 1),
+    ("ev", "A", 2, 1),
+    ("m2", "T", 2, 2, 1),
     ("ev", "V", 2, 2),
+    ("m2", "T", 2, 3, 1),
     ("ev", "A", 2, 3),
 ]
 
 CH = [512,256,256]
-LOADS = ["x0","zs","z1","x1","W","z0","x2","x3","o0","o1"]
+LOADS = ["x0","z1","zs","x1","W","z0","x2","x3","o0","o1"]
 I4 = True
 START = [sum(CH[:q]) for q in range(len(CH))]
 ZW = 256

from contextlib import ExitStack

import concourse.mybir as mybir
from concourse.masks import make_identity

N, M, K, L = 1024, 1024, 512, 1024
FLOPS = 2 * N * M * K + 2 * L * M * N

F32 = mybir.dt.float32
BF16 = mybir.dt.bfloat16
I32 = mybir.dt.int32
U32 = mybir.dt.uint32
U8 = mybir.dt.uint8
FP8 = mybir.dt.float8_e4m3fn
FP8X4 = mybir.dt.float8_e4m3fn_x4
FP4X4 = mybir.dt.float4_e2m1fn_x4
ALU = mybir.AluOpType
ACT = mybir.ActivationFunctionType

P = 128
T = 4
G = 2
HALF = 512
QUART = 256

PLAN = [
    ("dg", "V", 0),
    ("xt", "T", 0),
    ("dg", "V", 1),
    ("zw", "V", 1, 0),
    ("bs", "T"),
    ("xe", "A", 0),
    ("xq", "V", 0),
    ("xt", "T", 1),
    ("zw", "A", 1, 2),
    ("m1", "T", 0, 0),
    ("zw", "V", 1, 3),
    ("m1", "T", 0, 1),
    ("zw", "V", 1, 1),
    ("xe", "A", 1),
    ("ex", "A", 0, 0),
    ("m1", "T", 1, 0),
    ("m1", "T", 1, 1),
    ("zw", "V", 0, 0),
    ("xq", "V", 1),
    ("ex", "A", 0, 1),
    ("C", "V", 0),
    ("xt", "T", 2),
    ("m1", "T", 2, 0),
    ("zi", "P", 0, 0),
    ("ex", "A", 1, 0),
    ("ex", "A", 1, 1),
    ("xt", "T", 3),
    ("xe", "A", 2),
    ("C", "V", 1),
    ("m1", "T", 2, 1),
    ("xe", "A", 3),
    ("xq", "V", 2),
    ("ex", "A", 2, 0),
    ("m1", "T", 3, 0),
    ("ex", "A", 2, 1),
    ("ex", "A", 3, 0),
    ("m1", "T", 3, 1),
    ("zw", "V", 0, 1),
    ("xq", "V", 3),
    ("m1", "T", 4, 0),
    ("m1", "T", 4, 1),
    ("m1", "T", 5, 0),
    ("ex", "A", 3, 1),
    ("wo", "T", 0, 0, 0),
    ("ex", "A", 4, 0),
    ("ex", "A", 4, 1),
    ("zi", "P", 0, 1),
    ("m1", "T", 5, 1),
    ("ex", "A", 5, 0),
    ("ex", "A", 5, 1),
    ("zi", "P", 1, 0),
    ("C", "V", 2),
    ("m1", "T", 6, 0),
    ("ex", "A", 6, 0),
    ("m1", "T", 6, 1),
    ("C", "V", 3),
    ("wo", "T", 0, 0, 1),
    ("ex", "A", 6, 1),
    ("m1", "T", 7, 0),
    ("m1", "T", 7, 1),
    ("C", "V", 4),
    ("wo", "T", 0, 0, 2),
    ("a", "P", 0),
    ("ex", "A", 7, 0),
    ("ex", "A", 7, 1),
    ("zw", "A", 0, 2),
    ("C", "V", 5),
    ("C", "V", 6),
    ("C", "V", 7),
    ("a", "P", 1),
    ("zq", "V", 0, 0),
    ("D", "V", 0, 0, 0),
    ("zi", "A", 1, 2),
    ("wo", "T", 0, 0, 3),
    ("D", "V", 0, 0, 1),
    ("zw", "A", 0, 3),
    ("wo", "T", 0, 1, 0),
    ("D", "V", 0, 0, 2),
    ("zi", "A", 1, 1),
    ("wo", "T", 0, 1, 1),
    ("D", "V", 0, 0, 3),
    ("D", "V", 0, 1, 0),
    ("D", "V", 0, 1, 1),
    ("wo", "T", 0, 1, 2),
    ("wo", "T", 0, 1, 3),
    ("ri", "A", 0, 0, 0),
    ("D", "V", 0, 1, 2),
    ("wo", "T", 1, 0, 0),
    ("wo", "T", 1, 0, 1),
    ("D", "V", 0, 1, 3),
    ("ri", "A", 0, 0, 1),
    ("D", "V", 1, 0, 0),
    ("zi", "P", 0, 2),
    ("D", "V", 1, 0, 1),
    ("wo", "T", 1, 1, 0),
    ("ri", "A", 0, 1, 0),
    ("D", "V", 1, 1, 0),
    ("ri", "A", 0, 1, 1),
    ("zi", "P", 1, 3),
    ("wo", "T", 1, 1, 1),
    ("zq", "V", 1, 0),
    ("rq", "V", 0, 0),
    ("m2", "T", 0, 0, 0),
    ("wo", "T", 2, 0, 0),
    ("zq", "V", 0, 2),
    ("zq", "V", 0, 1),
    ("rq", "V", 0, 1),
    ("m2", "T", 0, 1, 0),
    ("wo", "T", 2, 0, 1),
    ("m2", "T", 0, 0, 1),
    ("m2", "T", 0, 2, 0),
    ("zq", "V", 1, 2),
    ("zq", "V", 1, 1),
    ("zi", "A", 0, 3),
    ("D", "V", 1, 1, 1),
    ("zq", "V", 1, 3),
    ("ri", "A", 1, 0, 0),
    ("ev", "A", 0, 0),
    ("rq", "V", 1, 0),
    ("m2", "T", 0, 1, 1),
    ("m2", "T", 0, 3, 0),
    ("m2", "T", 0, 2, 1),
    ("ri", "V", 1, 1, 0),
    ("ev", "A", 0, 1),
    ("m2", "T", 0, 4, 0),
    ("m2", "T", 0, 3, 1),
    ("m2", "T", 0, 5, 0),
    ("ev", "A", 0, 2),
    ("ev", "A", 0, 3),
    ("D", "V", 2, 0, 0),
    ("wo", "T", 2, 1, 0),
    ("rq", "V", 1, 1),
    ("m2", "T", 0, 4, 1),
    ("D", "V", 2, 0, 1),
    ("zq", "V", 0, 3),
    ("D", "V", 2, 1, 0),
    ("m2", "T", 0, 5, 1),
    ("wo", "T", 2, 1, 1),
    ("D", "V", 2, 1, 1),
    ("ri", "V", 2, 0, 0),
    ("ev", "A", 0, 4),
    ("m2", "T", 1, 0, 1),
    ("m2", "T", 1, 1, 1),
    ("ri", "V", 2, 1, 0),
    ("ev", "A", 0, 5),
    ("m2", "T", 0, 6, 0),
    ("m2", "T", 0, 6, 1),
    ("rq", "V", 2, 0),
    ("ev", "A", 1, 0),
    ("rq", "V", 2, 1),
    ("m2", "T", 0, 7, 0),
    ("ev", "A", 1, 1),
    ("m2", "T", 1, 2, 1),
    ("ev", "A", 0, 6),
    ("ev", "A", 1, 2),
    ("m2", "T", 0, 7, 1),
    ("m2", "T", 1, 3, 1),
    ("m2", "T", 2, 0, 1),
    ("ev", "A", 1, 3),
    ("ev", "V", 0, 7),
    ("m2", "T", 2, 1, 1),
    ("ev", "A", 2, 0),
    ("ev", "A", 2, 1),
    ("m2", "T", 2, 2, 1),
    ("ev", "V", 2, 2),
    ("m2", "T", 2, 3, 1),
    ("ev", "A", 2, 3),
]

CH = [512,256,256]
LOADS = ["x0","z1","zs","x1","W","z0","x2","x3","o0","o1"]
I4 = True
START = [sum(CH[:q]) for q in range(len(CH))]
ZW = 256


def tile_choosiowhalfsweepinstrumentmoments_d1p_kernel(
    tc, x, beta_words, beta_scales, bs, mass, obs, wt, z_bytes, z_scale, out
):
    nc = tc.nc
    with ExitStack() as ctx:
        ctx.enter_context(tc.manual_schedule())
        sb = ctx.enter_context(tc.tile_pool(name="sb", bufs=1))
        ps = ctx.enter_context(tc.psum_pool(name="ps", bufs=1))

        def sbuf(name, shape, dtype):
            return sb.tile(shape, dtype, name=name, align_bytes=64)

        def bank(index, name, shape, dtype):
            return ps.tile(shape, dtype, name=name, tag="bank%d" % index)

        w_scales = sbuf("w_scales", [P, M], U8)
        bs_row = sbuf("bs_row", [P, M], BF16)
        ones = sbuf("ones", [P, P], BF16)
        halves = sbuf("halves", [P, T], F32)
        warm = sbuf("warm", [P, 1], F32)
        ident = sbuf("ident", [P, P], F32)
        nc.vector.memset(w_scales[:].bitcast(I32), 0)
        nc.vector.memset(bs_row[:].bitcast(I32), 0)
        nc.vector.memset(ones[:], 1.0)
        nc.vector.memset(halves[:], 0.5)

        zs = sbuf("zs", [P, G, T * 8], F32)
        zb = {}
        xs = {}
        ob = {}
        w_words = sbuf("w_words", [P, 2 * M], U8)
        mass_sb = sbuf("mass_sb", [P, G, T], BF16)
        wt_sb = sbuf("wt_sb", [P, G, T], BF16)
        z_view = z_bytes.rearrange("(g p t) l -> g p (t l)", p=P, t=T)
        x_view = x.rearrange("(g p t) k -> g p (t k)", p=P, t=T)
        obs_view = obs.rearrange("(g p t) m -> g p (t m)", p=P, t=T)

        def load_z(g):
            zb[g] = sbuf("zb%d" % g, [P, T * L], U8)
            nc.sync.dma_start(out=zb[g][:], in_=z_view[g])

        def load_x(b):
            xs[b] = sbuf("xs%d" % b, [P, 2 * K], BF16)
            nc.sync.dma_start(out=xs[b][:], in_=x_view[b // 2][:, (b % 2) * 2 * K : (b % 2 + 1) * 2 * K])

        def load_obs(g):
            ob[g] = sbuf("ob%d" % g, [P, T * M], BF16)
            nc.sync.dma_start(out=ob[g][:], in_=obs_view[g])

        def load(name):
            if name == "zs":
                nc.sync.dma_start(out=zs[:], in_=z_scale.rearrange("(g p t) j -> p g (t j)", p=P, t=T))
            elif name == "W":
                nc.sync.dma_start(out=w_words[:].bitcast(I32), in_=beta_words[0].bitcast(I32))
            elif name[0] == "x":
                load_x(int(name[1]))
            elif name[0] == "o":
                load_obs(int(name[1]))
            else:
                load_z(int(name[1]))

        nc.scalar.dma_start(out=wt_sb[:], in_=wt.rearrange("(g p t) -> p g t", p=P, t=T))
        for name in LOADS[:3]:
            load(name)
        for q in range(4):
            nc.scalar.dma_start(
                out=w_scales[32 * q : 32 * q + 4, :].bitcast(I32),
                in_=beta_scales[0, 4 * q : 4 * q + 4, :].bitcast(I32),
            )
        nc.scalar.activation(out=warm[:], in_=halves[:, 0:1], func=ACT.Exp)
        make_identity(nc, ident[:])
        nc.gpsimd.dma_start(out=bs_row[0:1, :], in_=bs.rearrange("(o m) -> o m", o=1))
        nc.gpsimd.dma_start(out=mass_sb[:], in_=mass.rearrange("(g p t) -> p g t", p=P, t=T))
        for name in LOADS[3:]:
            load(name)
        wt_big = sbuf("wt_big", [P, G, T], F32)
        nc.gpsimd.tensor_scalar(
            out=wt_big[:], in0=wt_sb[:], scalar1=2048.0, scalar2=0.0, op0=ALU.mult, op1=ALU.add
        )

        t = {}
        count = {"wo": 0, "acc": 0}
        WO_BANKS = (7, 1, 2)
        ACC_BANKS = (3, 4, 5, 6, 0)

        def copy(eng, out_ap, in_ap):
            if eng == "A":
                nc.scalar.copy(out=out_ap, in_=in_ap)
            elif eng == "P":
                nc.gpsimd.tensor_scalar(out=out_ap, in0=in_ap, scalar1=1.0, scalar2=0.0, op0=ALU.mult, op1=ALU.add)
            else:
                nc.vector.tensor_copy(out=out_ap, in_=in_ap)

        def interleave(eng, dst, src):
            if I4 and eng != "P":
                copy(eng, dst.rearrange("p (c i) t -> p c t i", i=4), src.rearrange("p t (c i) -> p c t i", i=4))
            else:
                copy(eng, dst, src.rearrange("p t c -> p c t"))

        def zw(eng, g, u):
            wide = sbuf("zw%d%d" % (g, u), [P, T, ZW], BF16)
            t["zw", g, u] = wide
            for s in range(T):
                for jj in range(2):
                    j = 2 * u + jj
                    c0 = s * L + j * P
                    src = zb[g][:, c0 : c0 + P].bitcast(FP8)
                    scale = zs[:, g, 8 * s + j : 8 * s + j + 1]
                    dst = wide[:, s, jj * P : (jj + 1) * P]
                    if eng == "A":
                        nc.scalar.activation(out=dst, in_=src, func=ACT.Copy, scale=scale)
                    else:
                        nc.vector.tensor_scalar(out=dst, in0=src, scalar1=scale, scalar2=None, op0=ALU.mult)

        def zi(eng, g, u):
            grouped = sbuf("zi%d%d" % (g, u), [P, ZW, T], BF16)
            t["zi", g, u] = grouped
            interleave(eng, grouped[:], t["zw", g, u][:])

        def quantize(key, grouped, width):
            codes = sbuf("c" + key, [P, width], U32)
            scales = sbuf("s" + key, [P, width], U8)
            nc.vector.quantize_mx(out=codes[:].bitcast(FP8X4), scales=scales[:], in_=grouped)
            return codes, scales

        def zq(eng, g, j):
            t["zq", g, j] = quantize("z%d%d" % (g, j), t["zi", g, j][:].rearrange("p c t -> p (c t)"), ZW)

        def xt(eng, b):
            turned = bank(1 + b % 2, "xt%d" % b, [P, 2, 2, P], F32)
            t["xt", b] = turned
            words = xs[b][:].bitcast(F32)
            for a in range(2):
                w0 = 256 * a
                for u in range(2):
                    nc.tensor.transpose(turned[:, a, u, :], words[:, w0 + u : w0 + 256 : 2], ident[:])

        def xe(eng, b):
            grouped = sbuf("xe%d" % b, [P, 2 * P * T], BF16)
            t["xe", b] = grouped
            copy(
                eng,
                grouped[:].bitcast(F32).rearrange("p (a r u) -> p a r u", a=2, u=2),
                t["xt", b][:].rearrange("p a u r -> p a r u"),
            )

        def xq(eng, b):
            t["xq", b] = quantize("x%d" % b, t["xe", b][:], 2 * P)

        def bsb(eng):
            spread = bank(0, "bs_spread", [P, M], BF16)
            t["bs"] = spread
            for h in range(2):
                cols = slice(h * HALF, (h + 1) * HALF)
                nc.tensor.matmul(spread[:, cols], lhsT=ones[:], rhs=bs_row[:, cols], start=True, stop=True)

        def m1(eng, s, h):
            phi = bank(3 + (2 * s + h) % 4, "phi%d%d" % (s, h), [P, HALF], F32)
            t["phi", s, h] = phi
            codes, scales = t["xq", s // 2]
            cols = slice((s % 2) * P, (s % 2 + 1) * P)
            nc.tensor.matmul_mx(
                out=phi[:],
                lhsT=codes[:, cols].bitcast(FP8X4),
                lhsT_scale=scales[:, cols],
                rhs=w_words[:, 2 * h * HALF : 2 * (h + 1) * HALF].bitcast(FP4X4),
                rhs_scale=w_scales[:, h * HALF : (h + 1) * HALF],
                start=True,
                stop=True,
            )

        def ex(eng, s, h):
            if h == 0:
                t["E", s] = sbuf("E%d" % s, [P, M], F32)
            nc.scalar.activation(
                out=t["E", s][:, h * HALF : (h + 1) * HALF], in_=t["phi", s, h][:], func=ACT.Exp, scale=0.5
            )

        def cc(eng, s):
            if s % T == 0:
                t["hs", s // T] = sbuf("hs%d" % (s // T), [P, T], F32)
            t["e", s] = sbuf("e%d" % s, [P, M], F32)
            nc.vector.scalar_tensor_tensor(
                out=t["e", s][:],
                in0=t["E", s][:],
                scalar=1.0 / 2048.0,
                in1=t["bs"][:],
                op0=ALU.mult,
                op1=ALU.mult,
                accum_out=t["hs", s // T][:, s % T : s % T + 1],
            )

        def small(key, g):
            t[key, g] = sbuf("%s%d" % (key, g), [P, T], F32)
            return t[key, g][:]

        def y1(eng, g):
            nc.vector.tensor_tensor(out=small("sq", g), in0=t["hs", g][:], in1=t["hs", g][:], op=ALU.mult)

        def y2(eng, g):
            nc.vector.tensor_tensor(out=small("y", g), in0=t["sq", g][:], in1=mass_sb[:, g, :], op=ALU.add)

        def pw(eng, g):
            nc.gpsimd.tensor_tensor(out=small("root", g), in0=t["y", g][:], in1=halves[:], op=ALU.pow)

        def c1(eng, g):
            nc.vector.tensor_tensor(out=small("nega", g), in0=t["hs", g][:], in1=t["root", g][:], op=ALU.subtract)

        def aa(eng, g):
            if eng == "P":
                hs = t["hs", g]
                nc.gpsimd.tensor_tensor(out=small("sq", g), in0=hs[:], in1=hs[:], op=ALU.mult)
                nc.gpsimd.tensor_tensor(out=small("y", g), in0=t["sq", g][:], in1=mass_sb[:, g, :], op=ALU.add)
                pw(eng, g)
                nc.gpsimd.tensor_tensor(out=small("nega", g), in0=hs[:], in1=t["root", g][:], op=ALU.subtract)
                nc.gpsimd.tensor_tensor(out=small("coef", g), in0=t["nega", g][:], in1=wt_big[:, g, :], op=ALU.mult)
            else:
                nc.vector.tensor_tensor(out=small("coef", g), in0=t["nega", g][:], in1=wt_big[:, g, :], op=ALU.mult)

        def dg(eng, g):
            diag = sbuf("diag%d" % g, [P, T, P], BF16)
            t["dg", g] = diag
            for s in range(T):
                nc.vector.tensor_scalar(
                    out=diag[:, s, :], in0=ident[:], scalar1=wt_sb[:, g, s : s + 1], scalar2=None, op0=ALU.mult
                )

        def wo(eng, q, g, b):
            w = CH[q]
            per = HALF // w
            prod = bank(WO_BANKS[count["wo"] % 3], "wo%d%d%d" % (q, g, b), [P, per, w], F32)
            count["wo"] += 1
            t["wo", q, g, b] = prod
            for i in range(per):
                s = b * per + i
                c0 = s * M + START[q]
                nc.tensor.matmul(prod[:, i, :], lhsT=t["dg", g][:, s, :], rhs=ob[g][:, c0 : c0 + w], start=True, stop=True)

        def dd(eng, q, g, b):
            w = CH[q]
            per = HALF // w
            if b == 0:
                t["res", q, g] = sbuf("res%d%d" % (q, g), [P, T, w], BF16)
            for i in range(per):
                s = b * per + i
                nc.vector.scalar_tensor_tensor(
                    out=t["res", q, g][:, s, :],
                    in0=t["e", T * g + s][:, START[q] : START[q] + w],
                    scalar=t["coef", g][:, s : s + 1],
                    in1=t["wo", q, g, b][:, i, :],
                    op0=ALU.mult,
                    op1=ALU.add,
                )

        def ri(eng, q, g, i):
            w = CH[q]
            if ("ri", q, g) not in t:
                t["ri", q, g] = sbuf("ri%d%d" % (q, g), [P, w, T], BF16)
            cols = slice(i * QUART, min(w, (i + 1) * QUART))
            interleave(eng, t["ri", q, g][:, cols, :], t["res", q, g][:, :, cols])

        def rq(eng, q, g):
            t["rq", q, g] = quantize("r%d%d" % (q, g), t["ri", q, g][:].rearrange("p c t -> p (c t)"), CH[q])

        def m2(eng, q, b, g):
            w = CH[q]
            per = HALF // w
            if g == 0 or per > 1:
                t["acc", q, b] = bank(ACC_BANKS[count["acc"] % 5], "acc%d%d" % (q, b), [P, per, w], F32)
                count["acc"] += 1
            for i in range(per):
                j = b * per + i
                cols = slice((j % 2) * P, (j % 2 + 1) * P)
                for gg in ([g] if per == 1 else range(G)):
                    z_codes, z_scales = t["zq", gg, j // 2]
                    r_codes, r_scales = t["rq", q, gg]
                    nc.tensor.matmul_mx(
                        out=t["acc", q, b][:, i, :],
                        lhsT=z_codes[:, cols].bitcast(FP8X4),
                        lhsT_scale=z_scales[:, cols],
                        rhs=r_codes[:].bitcast(FP8X4),
                        rhs_scale=r_scales[:],
                        start=(gg == 0),
                        stop=(gg == G - 1),
                    )

        def ev(eng, q, b):
            w = CH[q]
            per = HALF // w
            result = sbuf("out%d%d" % (q, b), [P, per, w], F32)
            copy(eng, result[:], t["acc", q, b][:])
            rows = out[b * per * P : (b + 1) * per * P, START[q] : START[q] + w]
            nc.sync.dma_start(out=rows.rearrange("(i l) m -> l i m", l=P), in_=result[:])

        steps = {
            "zw": zw, "zi": zi, "zq": zq, "xt": xt, "xe": xe, "xq": xq, "bs": bsb, "m1": m1, "ex": ex,
            "C": cc, "a": aa, "y1": y1, "y2": y2, "pw": pw, "c1": c1, "dg": dg, "wo": wo, "D": dd, "ri": ri, "rq": rq, "m2": m2, "ev": ev,
        }
        for step in PLAN:
            steps[step[0]](*step[1:])
